import numpy as np
import ml_dtypes


def mxq(x, axis, fmt="e4m3"):
    dtype, down = {"e4m3": (ml_dtypes.float8_e4m3fn, 7), "e5m2": (ml_dtypes.float8_e5m2, 14)}[fmt]
    v = np.moveaxis(np.asarray(x, np.float32).astype(ml_dtypes.bfloat16).astype(np.float64), axis, -1)
    blocks = v.reshape(v.shape[:-1] + (-1, 32))
    amax = np.abs(blocks).max(-1, keepdims=True)
    byte = np.maximum(np.where(amax > 0, np.frexp(amax)[1] - 1 + 127, 0) - down, 1)
    scale = np.exp2(byte - 127.0)
    codes = (blocks / scale).astype(np.float32).astype(dtype).astype(np.float64)
    return np.moveaxis((codes * scale).reshape(v.shape), -1, axis)


WIDE = False


def mx_kscale(k):
    if not WIDE:
        return np.ones(k)
    levels = np.array([10, -10, 5, -5, 0])
    if k % 512:
        return np.exp2(np.random.permutation(np.resize(levels, k // 32))).repeat(32)
    a = np.empty((k // 512, 16))
    for p in range(k // 512):
        a[p, :8] = np.random.permutation(np.resize(levels, 8))
        for g in range(8):
            far = levels[np.abs(levels - a[p, g]) >= 10]
            a[p, g + 8] = far[np.random.randint(len(far))]
    return np.exp2(a.ravel()).repeat(32)


def f64(x):
    return np.asarray(x).astype(np.float64)


def striped(idx):
    return np.tile(np.asarray(idx).reshape(-1, 16).T, (8, 1)).astype(np.uint16)


def unstriped(offs):
    return offs[:16].T.reshape(-1).astype(np.int64)


E2M1 = np.array([0.0, 0.5, 1.0, 1.5, 2.0, 3.0, 4.0, 6.0, -0.0, -0.5, -1.0, -1.5, -2.0, -3.0, -4.0, -6.0])


def pack_weight(w, fmt):
    k, n = w.shape
    w = f64(np.asarray(w, np.float32).astype(ml_dtypes.bfloat16)).reshape(k // 32, 32, n)
    amax = np.abs(w).max(1)
    if fmt == "e4m3":
        byte = np.frexp(amax)[1] - 1 + 127 - 7
    else:
        mant, ex = np.frexp(amax / 6.0)
        byte = np.where(mant > 0.5, ex, ex - 1) + 127
    byte = np.clip(np.where(amax > 0, byte, 1), 1, 254)
    scaled = (w * np.exp2(127.0 - byte)[:, None, :]).reshape(k, n).astype(np.float32)
    by_word = np.ascontiguousarray(scaled.reshape(k // 512, 128, 4, n).transpose(0, 1, 3, 2))
    if fmt == "e4m3":
        words = by_word.astype(ml_dtypes.float8_e4m3fn).view(np.uint8)
    else:
        c = by_word.astype(ml_dtypes.float4_e2m1fn).view(np.uint8) & 0xF
        words = (c[..., 0::2] | (c[..., 1::2] << 4)).reshape(k // 512, 128, 2 * n)
    return np.ascontiguousarray(words), np.ascontiguousarray(byte.astype(np.uint8).reshape(k // 512, 16, n))


def unpack_weight(words, scales, fmt):
    g, _, n = scales.shape
    words = np.ascontiguousarray(words).reshape(g, 128, n, -1)
    if fmt == "e4m3":
        vals = words.view(ml_dtypes.float8_e4m3fn).astype(np.float64)
    else:
        nib = np.empty((g, 128, n, 4), np.uint8)
        nib[..., 0::2] = words & 0xF
        nib[..., 1::2] = words >> 4
        vals = E2M1[nib]
    vals = vals * np.repeat(np.exp2(scales.astype(np.float64) - 127.0), 8, axis=1)[..., None]
    return vals.transpose(0, 1, 3, 2).reshape(g * 512, n)


def softplus(v):
    return np.log(1.0 + np.exp(v))


def sigmoid(v):
    return 1.0 / (1.0 + np.exp(-v))


D, T, U, I, J, G = 512, 1024, 1024, 256, 512, 64


def setup_inputs():
    n = np.random.standard_normal
    idx = np.random.permutation(T)[:I]
    idx2 = np.random.permutation(U)[:J]
    fd = mx_kscale(D)
    tabbp = pack_weight(n((D, U)) / fd[:, None], "e2m1")
    return {
        "taba": (n((D, T)) * 1 / np.sqrt(D) * fd[:, None]).astype(np.float32),
        "dtab": (n((D, T)) * 1.3 / np.sqrt(D) * fd[:, None]).astype(np.float32),
        "tabb_words": tabbp[0],
        "tabb_scales": tabbp[1],
        "reserve": (np.random.uniform(20.0, 100.0, (I, 1))).astype(np.float32),
        "stake": (n((I, G)) * 1.5).astype(np.float32),
        "base": (0.3 * n((I, J))).astype(np.float32),
        "offs": striped(idx),
        "offs2": striped(idx2),
    }


def reference(taba, dtab, tabb_words, tabb_scales, reserve, stake, base, offs, offs2):
    idx = unstriped(offs)
    idx2 = unstriped(offs2)
    tabbu = unpack_weight(tabb_words, tabb_scales, "e2m1")
    tabaidxq = mxq(f64(taba)[:, idx], 0, "e4m3")
    tabbidx2g = tabbu[:, idx2]
    s = tabaidxq.T @ tabbidx2g
    dtabidxq = mxq(f64(dtab)[:, idx], 0, "e4m3")
    ts = dtabidxq.T @ tabbidx2g
    p = softplus(s)
    z = np.sum(p, axis=1, keepdims=True) + f64(reserve)
    s1g = p.reshape(I, G, J // G).sum(axis=2) / z
    ds1g = f64(stake) / (s1g * 64.0 + 1.0) * 64.0
    e1 = ds1g / z
    r1 = np.repeat(e1, J // G, axis=1)
    dz = np.sum(ds1g * p.reshape(I, G, J // G).sum(axis=2) / np.square(z) * (-1.0), axis=1, keepdims=True)
    dp = r1 + dz
    xp = ts * sigmoid(s)
    xz = np.sum(xp, axis=1, keepdims=True)
    xs1g = (xp.reshape(I, G, J // G).sum(axis=2) - xz * p.reshape(I, G, J // G).sum(axis=2) / z) / z
    xds1g = xs1g * 64.0 * f64(stake) / np.square(s1g * 64.0 + 1.0) * (-1.0) * 64.0
    xe1 = (xds1g - xz * ds1g / z) / z
    xr1 = np.repeat(xe1, J // G, axis=1)
    xdz = np.sum((xds1g * p.reshape(I, G, J // G).sum(axis=2) + xp.reshape(I, G, J // G).sum(axis=2) * ds1g - xz * z * 2.0 * ds1g * p.reshape(I, G, J // G).sum(axis=2) / np.square(z)) / np.square(z) * (-1.0), axis=1, keepdims=True)
    xdp = xr1 + xdz
    xds = xdp * sigmoid(s) + ts * sigmoid(s) * (1.0 - sigmoid(s)) * dp
    y = xds * 8.0 + f64(base)
    return y

@@ -1,0 +1,166 @@
+from contextlib import ExitStack
+
+import concourse.mybir as mybir
+
+D, T, U, I, J, G = 512, 1024, 1024, 256, 512, 64
+FLOPS = 2 * 2 * D * I * J
+
+F32 = mybir.dt.float32
+BF16 = mybir.dt.bfloat16
+I32 = mybir.dt.int32
+U32 = mybir.dt.uint32
+U16 = mybir.dt.uint16
+U8 = mybir.dt.uint8
+FP8X4 = mybir.dt.float8_e4m3fn_x4
+FP4X4 = mybir.dt.float4_e2m1fn_x4
+ALU = mybir.AluOpType
+ACT = mybir.ActivationFunctionType
+AX = mybir.AxisListType
+
+P = 128
+PACK = 4
+TILES = I // P
+GW = J // G
+LN_FLOOR = 2.0 ** -62
+
+
+def tile_attend_hvpairquota_kernel(tc, taba, dtab, tabb_words, tabb_scales, reserve, stake, base, offs, offs2, out):
+    nc = tc.nc
+    with ExitStack() as ctx:
+        keep = ctx.enter_context(tc.tile_pool(name="keep", bufs=1))
+        psum = ctx.enter_context(tc.psum_pool(name="psum", bufs=1))
+
+        def grouped(ap):
+            return ap.rearrange("p (g r) -> p g r", r=GW)
+
+        def spread(ap):
+            return ap.unsqueeze(2).to_broadcast([P, G, GW])
+
+        list_b = keep.tile([P, J // 16], U16, name="list_b")
+        nc.sync.dma_start(list_b[:], offs2)
+        words = keep.tile([P, U], U16, name="words", align_bytes=64)
+        nc.sync.dma_start(words[:].bitcast(I32), tabb_words[0].bitcast(I32))
+        list_a = keep.tile([P, I // 16], U16, name="list_a")
+        nc.sync.dma_start(list_a[:], offs)
+
+        planes = {}
+        for name, table in (("a", taba), ("d", dtab)):
+            rows = table.rearrange("(p t) c -> t p c", t=PACK)
+            for t in range(PACK):
+                planes[name, t] = keep.tile([P, T], F32, name=f"plane_{name}{t}")
+                nc.sync.dma_start(planes[name, t][:], rows[t])
+        base_sb = [keep.tile([P, J], F32, name=f"base{m}") for m in range(TILES)]
+        for m in range(TILES):
+            nc.sync.dma_start(base_sb[m][:], base[m * P : (m + 1) * P, :])
+
+        scales = keep.tile([P, U], U8, name="scales", align_bytes=64)
+        nc.gpsimd.memset(scales[:].bitcast(I32), 0)
+        for quad in range(4):
+            nc.gpsimd.dma_start(
+                scales[32 * quad : 32 * quad + 4, :].bitcast(I32),
+                tabb_scales[0, 4 * quad : 4 * quad + 4, :].bitcast(I32),
+            )
+        stake_sb = keep.tile([P, TILES, G], F32, name="stake_sb")
+        nc.gpsimd.dma_start(stake_sb[:], stake.rearrange("(m p) g -> p m g", p=P))
+        reserve_sb = keep.tile([P, TILES], F32, name="reserve_sb")
+        with nc.allow_non_contiguous_dma(reason="one reserve a partition and tile"):
+            nc.gpsimd.dma_start(reserve_sb[:].unsqueeze(2), reserve.rearrange("(m p) o -> p m o", p=P))
+
+        pair = keep.tile([P, TILES, 2], F32, name="pair")
+        nc.vector.memset(pair[:], 1.0 / 64.0)
+        floor = keep.tile([P, 1], F32, name="floor")
+        nc.vector.memset(floor[:], LN_FLOOR)
+        warm = keep.tile([P, 1], F32, name="warm")
+        nc.scalar.activation(warm[:], pair[:, 0, 0:1], ACT.Sigmoid)
+
+        b_words = keep.tile([P, J], U16, name="b_words", align_bytes=64)
+        nc.vector.tensor_copy(b_words[:], words[:].indirect(list_b[:]))
+        b_scales = keep.tile([P, J], U8, name="b_scales", align_bytes=64)
+
+        def gather(name, woven, t):
+            nc.vector.tensor_copy(woven[:, :, t], planes[name, t][:].indirect(list_a[:]))
+
+        def scores(name, woven):
+            codes = keep.tile([P, I], U32, name=f"codes_{name}", align_bytes=64)
+            plane = keep.tile([P, I], U8, name=f"scale_{name}", align_bytes=64)
+            nc.vector.quantize_mx(out=codes[:].bitcast(FP8X4), scales=plane[:], in_=woven[:].rearrange("p c t -> p (c t)"))
+            banks = []
+            for m in range(TILES):
+                bank = psum.tile([P, J], F32, name=f"bank_{name}{m}")
+                cols = slice(m * P, (m + 1) * P)
+                nc.tensor.matmul_mx(
+                    out=bank[:], lhsT=codes[:, cols].bitcast(FP8X4), lhsT_scale=plane[:, cols],
+                    rhs=b_words[:].bitcast(FP4X4), rhs_scale=b_scales[:], start=True, stop=True,
+                )
+                banks.append(bank)
+            return banks
+
+        woven_a = keep.tile([P, I, PACK], BF16, name="woven_a", align_bytes=64)
+        woven_d = keep.tile([P, I, PACK], BF16, name="woven_d", align_bytes=64)
+        gather("a", woven_a, 0)
+        nc.vector.tensor_copy(b_scales[:], scales[:].indirect(list_b[:]))
+        stake_sum = keep.tile([P, TILES], F32, name="stake_sum")
+        nc.vector.tensor_reduce(stake_sum[:], stake_sb[:], AX.X, ALU.add)
+        for t in range(1, PACK):
+            gather("a", woven_a, t)
+        s = scores("a", woven_a)
+
+        def big(name):
+            return [keep.tile([P, J], F32, name=f"{name}{m}") for m in range(TILES)]
+
+        def small(name):
+            return [keep.tile([P, G], F32, name=f"{name}{m}") for m in range(TILES)]
+
+        def col(name):
+            return keep.tile([P, TILES], F32, name=name)
+
+        q, lnq, sig = big("q"), big("lnq"), big("sig")
+        for m in range(TILES):
+            nc.scalar.activation(q[m][:], s[m][:], ACT.Sigmoid, scale=-1.0)
+        for m in range(TILES):
+            nc.scalar.activation(lnq[m][:], q[m][:], ACT.Ln, bias=floor[:])
+        for m in range(TILES):
+            nc.scalar.activation(sig[m][:], q[m][:], ACT.Copy, scale=-1.0, bias=1.0)
+
+        for t in range(PACK):
+            gather("d", woven_d, t)
+        ts = scores("d", woven_d)
+
+        p, xpn, hn, yn, u, v, o = big("p"), big("xpn"), big("hn"), big("yn"), big("u"), big("v"), big("o")
+        pg, den, rec, e1, f64, xg, t0 = small("pg"), small("den"), small("rec"), small("e1"), small("f64"), small("xg"), small("t0")
+        p_sum, z, zi, gz, e1_sum, c1, xzn, t0_sum, y_row = (
+            col("p_sum"), col("z"), col("zi"), col("gz"), col("e1_sum"), col("c1"), col("xzn"), col("t0_sum"), col("y_row"))
+        xpair = keep.tile([P, TILES, 2], F32, name="xpair")
+
+        for m in range(TILES):
+            nc.vector.scalar_tensor_tensor(p[m][:], lnq[m][:], -1.0, s[m][:], ALU.mult, ALU.max, accum_out=p_sum[:, m : m + 1])
+        nc.vector.tensor_reduce(pg[0][:], grouped(p[0][:]), AX.X, ALU.add)
+        nc.vector.tensor_tensor(z[:], p_sum[:], reserve_sb[:], ALU.add)
+        nc.vector.tensor_reduce(pg[1][:], grouped(p[1][:]), AX.X, ALU.add)
+        for m in range(TILES):
+            nc.vector.tensor_scalar(den[m][:], pg[m][:], 64.0, z[:, m : m + 1], ALU.mult, ALU.add)
+        nc.vector.reciprocal(zi[:], z[:])
+        for m in range(TILES):
+            nc.vector.reciprocal(rec[m][:], den[m][:])
+        nc.vector.scalar_tensor_tensor(gz[:], stake_sum[:], 8.0, zi[:], ALU.mult, ALU.mult)
+        for m in range(TILES):
+            nc.vector.scalar_tensor_tensor(e1[m][:], stake_sb[:, m, :], 512.0, rec[m][:], ALU.mult, ALU.mult, accum_out=e1_sum[:, m : m + 1])
+        nc.vector.scalar_tensor_tensor(pair[:, :, 1], gz[:], -1.0, zi[:], ALU.mult, ALU.mult)
+        for m in range(TILES):
+            nc.vector.scalar_tensor_tensor(xpn[m][:], q[m][:], 1.0, ts[m][:], ALU.subtract, ALU.mult, accum_out=xzn[:, m : m + 1])
+            nc.vector.scalar_tensor_tensor(f64[m][:], e1[m][:], 64.0, rec[m][:], ALU.mult, ALU.mult)
+        nc.vector.scalar_tensor_tensor(c1[:], e1_sum[:], -1.0 / 64.0, gz[:], ALU.mult, ALU.add)
+        for m in range(TILES):
+            nc.vector.tensor_reduce(xg[m][:], grouped(xpn[m][:]), AX.X, ALU.add)
+            nc.vector.tensor_scalar(xpair[:, m, :], pair[:, m, :], xzn[:, m : m + 1], None, ALU.mult)
+        for m in range(TILES):
+            nc.vector.tensor_tensor(hn[m][:], xpn[m][:], q[m][:], ALU.mult)
+            nc.vector.scalar_tensor_tensor(t0[m][:], xg[m][:], xpair[:, m, 0:1], f64[m][:], ALU.add, ALU.mult, accum_out=t0_sum[:, m : m + 1])
+        for m in range(TILES):
+            nc.vector.scalar_tensor_tensor(grouped(yn[m][:]), spread(e1[m][:]), c1[:, m : m + 1], grouped(hn[m][:]), ALU.subtract, ALU.mult)
+            nc.vector.tensor_scalar(y_row[:, m : m + 1], t0_sum[:, m : m + 1], 1.0 / 64.0, xpair[:, m, 1:2], ALU.mult, ALU.add)
+        for m in range(TILES):
+            nc.vector.tensor_tensor(u[m][:], base_sb[m][:], yn[m][:], ALU.subtract)
+            nc.vector.scalar_tensor_tensor(grouped(v[m][:]), spread(t0[m][:]), y_row[:, m : m + 1], grouped(sig[m][:]), ALU.add, ALU.mult)
+            nc.vector.tensor_tensor(o[m][:], v[m][:], u[m][:], ALU.add)
+            nc.sync.dma_start(out[m * P : (m + 1) * P, :], o[m][:])

@@ -1,6 +1,7 @@
 from contextlib import ExitStack
 
 import concourse.mybir as mybir
+from concourse.masks import make_identity
 
 D, T, U, I, J, G = 512, 1024, 1024, 256, 512, 64
 FLOPS = 2 * 2 * D * I * J
@@ -20,7 +21,8 @@ AX = mybir.AxisListType
 P = 128
 PACK = 4
 TILES = I // P
-GW = J // G
+BLOCKS = J // P
+HALF = P // G
 LN_FLOOR = 2.0 ** -62
 
 
@@ -30,11 +32,8 @@ def tile_attend_hvpairquota_kernel(tc, taba, dtab, tabb_words, tabb_scales, rese
         keep = ctx.enter_context(tc.tile_pool(name="keep", bufs=1))
         psum = ctx.enter_context(tc.psum_pool(name="psum", bufs=1))
 
-        def grouped(ap):
-            return ap.rearrange("p (g r) -> p g r", r=GW)
-
-        def spread(ap):
-            return ap.unsqueeze(2).to_broadcast([P, G, GW])
+        scales = keep.tile([P, U], U8, name="scales", align_bytes=64)
+        nc.gpsimd.memset(scales[:].bitcast(I32), 0)
 
         list_b = keep.tile([P, J // 16], U16, name="list_b")
         nc.sync.dma_start(list_b[:], offs2)
@@ -43,124 +42,178 @@ def tile_attend_hvpairquota_kernel(tc, taba, dtab, tabb_words, tabb_scales, rese
         list_a = keep.tile([P, I // 16], U16, name="list_a")
         nc.sync.dma_start(list_a[:], offs)
 
+        for quad in range(4):
+            nc.sync.dma_start(
+                scales[32 * quad : 32 * quad + 4, :].bitcast(I32),
+                tabb_scales[0, 4 * quad : 4 * quad + 4, :].bitcast(I32),
+            )
         planes = {}
-        for name, table in (("a", taba), ("d", dtab)):
-            rows = table.rearrange("(p t) c -> t p c", t=PACK)
-            for t in range(PACK):
-                planes[name, t] = keep.tile([P, T], F32, name=f"plane_{name}{t}")
-                nc.sync.dma_start(planes[name, t][:], rows[t])
+        rows_a = taba.rearrange("(p t) c -> p t c", t=PACK)
+        rows_d = dtab.rearrange("(p t) c -> p t c", t=PACK)
+        first_two = keep.tile([P, 2, T], F32, name="first_two")
+        nc.sync.dma_start(first_two[:], rows_a[:, 0:2, :])
+        planes["a", 0], planes["a", 1] = first_two[:, 0, :], first_two[:, 1, :]
+        stake_sb = keep.tile([P, TILES, G], F32, name="stake_sb")
+        nc.sync.dma_start(stake_sb[:], stake.rearrange("(m p) g -> p m g", p=P))
+        for name, rows, first in (("a", rows_a, 2), ("d", rows_d, 0)):
+            for t in range(first, PACK):
+                plane_tile = keep.tile([P, T], F32, name=f"plane_{name}{t}")
+                nc.sync.dma_start(plane_tile[:], rows[:, t, :])
+                planes[name, t] = plane_tile[:]
+        reserve_sb = keep.tile([P, TILES], F32, name="reserve_sb")
+        with nc.allow_non_contiguous_dma(reason="one reserve a partition and tile"):
+            nc.sync.dma_start(reserve_sb[:].unsqueeze(2), reserve.rearrange("(m p) o -> p m o", p=P))
         base_sb = [keep.tile([P, J], F32, name=f"base{m}") for m in range(TILES)]
         for m in range(TILES):
             nc.sync.dma_start(base_sb[m][:], base[m * P : (m + 1) * P, :])
 
-        scales = keep.tile([P, U], U8, name="scales", align_bytes=64)
-        nc.gpsimd.memset(scales[:].bitcast(I32), 0)
-        for quad in range(4):
-            nc.gpsimd.dma_start(
-                scales[32 * quad : 32 * quad + 4, :].bitcast(I32),
-                tabb_scales[0, 4 * quad : 4 * quad + 4, :].bitcast(I32),
-            )
-        stake_sb = keep.tile([P, TILES, G], F32, name="stake_sb")
-        nc.gpsimd.dma_start(stake_sb[:], stake.rearrange("(m p) g -> p m g", p=P))
-        reserve_sb = keep.tile([P, TILES], F32, name="reserve_sb")
-        with nc.allow_non_contiguous_dma(reason="one reserve a partition and tile"):
-            nc.gpsimd.dma_start(reserve_sb[:].unsqueeze(2), reserve.rearrange("(m p) o -> p m o", p=P))
+        ident = keep.tile([P, P], F32, name="ident")
+        make_identity(nc, ident[:])
 
-        pair = keep.tile([P, TILES, 2], F32, name="pair")
-        nc.vector.memset(pair[:], 1.0 / 64.0)
         floor = keep.tile([P, 1], F32, name="floor")
         nc.vector.memset(floor[:], LN_FLOOR)
-        warm = keep.tile([P, 1], F32, name="warm")
-        nc.scalar.activation(warm[:], pair[:, 0, 0:1], ACT.Sigmoid)
 
+        got_words = keep.tile([P, J], U16, name="got_words", align_bytes=64)
+        got_scales = keep.tile([P, J], U8, name="got_scales", align_bytes=64)
         b_words = keep.tile([P, J], U16, name="b_words", align_bytes=64)
-        nc.vector.tensor_copy(b_words[:], words[:].indirect(list_b[:]))
         b_scales = keep.tile([P, J], U8, name="b_scales", align_bytes=64)
 
-        def gather(name, woven, t):
-            nc.vector.tensor_copy(woven[:, :, t], planes[name, t][:].indirect(list_a[:]))
+        def deal(dst, src, run):
+            nc.vector.tensor_copy(
+                dst.rearrange("p (c b g) -> p b c g", c=BLOCKS, g=run), src.rearrange("p (b g c) -> p b c g", c=BLOCKS, g=run))
 
-        def scores(name, woven):
-            codes = keep.tile([P, I], U32, name=f"codes_{name}", align_bytes=64)
-            plane = keep.tile([P, I], U8, name=f"scale_{name}", align_bytes=64)
-            nc.vector.quantize_mx(out=codes[:].bitcast(FP8X4), scales=plane[:], in_=woven[:].rearrange("p c t -> p (c t)"))
-            banks = []
-            for m in range(TILES):
-                bank = psum.tile([P, J], F32, name=f"bank_{name}{m}")
-                cols = slice(m * P, (m + 1) * P)
+        def gather(name, woven, t, m=None):
+            if m is None:
+                nc.vector.tensor_copy(woven[:, :, t], planes[name, t].indirect(list_a[:]))
+            else:
+                nc.vector.tensor_copy(woven[:, m * P : (m + 1) * P, t], planes[name, t].indirect(list_a[:, m * 8 : (m + 1) * 8]))
+
+        def scores(name, woven, m):
+            codes = keep.tile([P, P], U32, name=f"codes_{name}{m}", align_bytes=64)
+            plane = keep.tile([P, P], U8, name=f"scale_{name}{m}", align_bytes=64)
+            nc.vector.quantize_mx(
+                out=codes[:].bitcast(FP8X4), scales=plane[:],
+                in_=woven[:, m * P : (m + 1) * P, :].rearrange("p c t -> p (c t)"))
+            bank = psum.tile([P, J], F32, name=f"bank_{name}{m}", tag=f"bank_{name}{m}")
+            for c in range(BLOCKS):
+                cols = slice(c * P, (c + 1) * P)
                 nc.tensor.matmul_mx(
-                    out=bank[:], lhsT=codes[:, cols].bitcast(FP8X4), lhsT_scale=plane[:, cols],
-                    rhs=b_words[:].bitcast(FP4X4), rhs_scale=b_scales[:], start=True, stop=True,
+                    out=bank[:, cols], lhsT=b_words[:, cols].bitcast(FP4X4), lhsT_scale=b_scales[:, cols],
+                    rhs=codes[:].bitcast(FP8X4), rhs_scale=plane[:], start=True, stop=True,
                 )
-                banks.append(bank)
-            return banks
+            return bank
 
         woven_a = keep.tile([P, I, PACK], BF16, name="woven_a", align_bytes=64)
-        woven_d = keep.tile([P, I, PACK], BF16, name="woven_d", align_bytes=64)
+        woven_d = keep.tile([P, I, PACK], BF16, name="woven_d", tag="woven_d", align_bytes=64)
+        nc.vector.tensor_copy(got_words[:], words[:].indirect(list_b[:]))
+        nc.vector.tensor_copy(got_scales[:], scales[:].indirect(list_b[:]))
+        deal(b_words[:].bitcast(I32), got_words[:].bitcast(I32), 4)
         gather("a", woven_a, 0)
-        nc.vector.tensor_copy(b_scales[:], scales[:].indirect(list_b[:]))
-        stake_sum = keep.tile([P, TILES], F32, name="stake_sum")
-        nc.vector.tensor_reduce(stake_sum[:], stake_sb[:], AX.X, ALU.add)
-        for t in range(1, PACK):
+        deal(b_scales[:].bitcast(U16), got_scales[:].bitcast(U16), 8)
+        for t in range(1, PACK - 1):
             gather("a", woven_a, t)
-        s = scores("a", woven_a)
+        for m in range(TILES):
+            gather("a", woven_a, PACK - 1, m)
+        s = [scores("a", woven_a, m) for m in range(TILES)]
 
-        def big(name):
-            return [keep.tile([P, J], F32, name=f"{name}{m}") for m in range(TILES)]
+        def tiles(name, width):
+            return [keep.tile([P, width], F32, name=f"{name}{m}", tag=f"{name}{m}") for m in range(TILES)]
 
-        def small(name):
-            return [keep.tile([P, G], F32, name=f"{name}{m}") for m in range(TILES)]
-
-        def col(name):
-            return keep.tile([P, TILES], F32, name=name)
-
-        q, lnq, sig = big("q"), big("lnq"), big("sig")
+        q, lnq = tiles("q", J), tiles("lnq", J)
+        stake8, stake8_sum = tiles("stake8", G), tiles("stake8_sum", 1)
+        for m in range(TILES):
+            nc.scalar.activation(stake8[m][:], stake_sb[:, m, :], ACT.Copy, scale=8.0, accum_out=stake8_sum[m][:])
         for m in range(TILES):
             nc.scalar.activation(q[m][:], s[m][:], ACT.Sigmoid, scale=-1.0)
         for m in range(TILES):
             nc.scalar.activation(lnq[m][:], q[m][:], ACT.Ln, bias=floor[:])
-        for m in range(TILES):
-            nc.scalar.activation(sig[m][:], q[m][:], ACT.Copy, scale=-1.0, bias=1.0)
 
-        for t in range(PACK):
+        for t in range(PACK - 1):
             gather("d", woven_d, t)
-        ts = scores("d", woven_d)
+        for m in range(TILES):
+            gather("d", woven_d, PACK - 1, m)
+        ts = [scores("d", woven_d, m) for m in range(TILES)]
 
-        p, xpn, hn, yn, u, v, o = big("p"), big("xpn"), big("hn"), big("yn"), big("u"), big("v"), big("o")
-        pg, den, rec, e1, f64, xg, t0 = small("pg"), small("den"), small("rec"), small("e1"), small("f64"), small("xg"), small("t0")
-        p_sum, z, zi, gz, e1_sum, c1, xzn, t0_sum, y_row = (
-            col("p_sum"), col("z"), col("zi"), col("gz"), col("e1_sum"), col("c1"), col("xzn"), col("t0_sum"), col("y_row"))
-        xpair = keep.tile([P, TILES, 2], F32, name="xpair")
+        def turn_sum(dst, src):
+            for c in range(BLOCKS):
+                nc.tensor.matmul(dst, src[:, c * P : (c + 1) * P], ident[:], start=(c == 0), stop=(c == BLOCKS - 1), is_transpose=True)
+
+        p_both = keep.tile([P, TILES, J], F32, name="p_both", tag="woven_d", align_bytes=64)
+        p = [p_both[:, m, :] for m in range(TILES)]
+        xpn, y, v, o = (tiles(n, J) for n in ("xpn", "y", "v", "o"))
+        p64, xh, dn2, tn2 = (tiles(n, P) for n in ("p64", "xh", "dn2", "tn2"))
+        den, rec = tiles("den", G + 1), tiles("rec", G + 1)
+        e1n, f64n, xs, t0 = (tiles(n, G) for n in ("e1n", "f64n", "xs", "t0"))
+        p64_sum, e1n_sum, gz, kk, cn, xzn, xzn64, kx, t0_sum, yn_row = (
+            tiles(n, 1) for n in ("p64_sum", "e1n_sum", "gz", "kk", "cn", "xzn", "xzn64", "kx", "t0_sum", "yn_row"))
+        p_pairs = [psum.tile([P, P], F32, name=f"p_pairs{m}") for m in range(TILES)]
+        x_pairs = [psum.tile([P, P], F32, name=f"x_pairs{m}", tag=f"acc{m}") for m in range(TILES)]
+        d_turned, t_turned = [], []
+
+        def twice(ap):
+            return ap.unsqueeze(2).to_broadcast([P, G, HALF])
+
+        def pairs(ap):
+            return ap.rearrange("p (g h) -> p g h", h=HALF)
+
+        def blocks(ap):
+            return ap.rearrange("p (c i) -> p c i", c=BLOCKS)
+
+        def each_block(ap):
+            return ap.unsqueeze(1).to_broadcast([P, BLOCKS, P])
 
         for m in range(TILES):
-            nc.vector.scalar_tensor_tensor(p[m][:], lnq[m][:], -1.0, s[m][:], ALU.mult, ALU.max, accum_out=p_sum[:, m : m + 1])
-        nc.vector.tensor_reduce(pg[0][:], grouped(p[0][:]), AX.X, ALU.add)
-        nc.vector.tensor_tensor(z[:], p_sum[:], reserve_sb[:], ALU.add)
-        nc.vector.tensor_reduce(pg[1][:], grouped(p[1][:]), AX.X, ALU.add)
+            nc.vector.scalar_tensor_tensor(p[m], lnq[m][:], -1.0, s[m][:], ALU.mult, ALU.max)
+            turn_sum(p_pairs[m][:], p[m])
         for m in range(TILES):
-            nc.vector.tensor_scalar(den[m][:], pg[m][:], 64.0, z[:, m : m + 1], ALU.mult, ALU.add)
-        nc.vector.reciprocal(zi[:], z[:])
+            nc.vector.scalar_tensor_tensor(xpn[m][:], q[m][:], 1.0, ts[m][:], ALU.subtract, ALU.mult)
+            turn_sum(x_pairs[m][:], xpn[m])
+        for m in range(TILES):
+            nc.scalar.activation(p64[m][:], p_pairs[m][:], ACT.Copy, scale=64.0, accum_out=p64_sum[m][:])
+            nc.scalar.activation(den[m][:, G : G + 1], p64_sum[m][:], ACT.Identity, scale=1.0 / 64.0, bias=reserve_sb[:, m : m + 1])
+            nc.vector.scalar_tensor_tensor(den[m][:, 0:G], p64[m][:, 0::2], den[m][:, G : G + 1], p64[m][:, 1::2], ALU.add, ALU.add)
         for m in range(TILES):
             nc.vector.reciprocal(rec[m][:], den[m][:])
-        nc.vector.scalar_tensor_tensor(gz[:], stake_sum[:], 8.0, zi[:], ALU.mult, ALU.mult)
         for m in range(TILES):
-            nc.vector.scalar_tensor_tensor(e1[m][:], stake_sb[:, m, :], 512.0, rec[m][:], ALU.mult, ALU.mult, accum_out=e1_sum[:, m : m + 1])
-        nc.vector.scalar_tensor_tensor(pair[:, :, 1], gz[:], -1.0, zi[:], ALU.mult, ALU.mult)
+            nc.scalar.activation(xh[m][:], x_pairs[m][:], ACT.Copy, accum_out=xzn[m][:])
+            nc.scalar.activation(xzn64[m][:], xzn[m][:], ACT.Copy, scale=1.0 / 64.0)
+            nc.vector.scalar_tensor_tensor(xs[m][:], xh[m][:, 0::2], xzn64[m][:], xh[m][:, 1::2], ALU.add, ALU.add)
         for m in range(TILES):
-            nc.vector.scalar_tensor_tensor(xpn[m][:], q[m][:], 1.0, ts[m][:], ALU.subtract, ALU.mult, accum_out=xzn[:, m : m + 1])
-            nc.vector.scalar_tensor_tensor(f64[m][:], e1[m][:], 64.0, rec[m][:], ALU.mult, ALU.mult)
-        nc.vector.scalar_tensor_tensor(c1[:], e1_sum[:], -1.0 / 64.0, gz[:], ALU.mult, ALU.add)
+            nc.vector.scalar_tensor_tensor(e1n[m][:], stake8[m][:], -64.0, rec[m][:, 0:G], ALU.mult, ALU.mult, accum_out=e1n_sum[m][:])
+            nc.scalar.activation(gz[m][:], stake8_sum[m][:], ACT.Copy, scale=rec[m][:, G : G + 1])
+            nc.scalar.activation(cn[m][:], e1n_sum[m][:], ACT.Identity, scale=1.0 / 64.0, bias=gz[m][:])
+            nc.scalar.activation(pairs(dn2[m][:]), twice(e1n[m][:]), ACT.Identity, bias=cn[m][:])
+            d_turned.append(psum.tile([P, P], F32, name=f"d_turned{m}", tag=f"bank_a{m}"))
+            nc.tensor.transpose(d_turned[m][:], dn2[m][:], ident[:])
         for m in range(TILES):
-            nc.vector.tensor_reduce(xg[m][:], grouped(xpn[m][:]), AX.X, ALU.add)
-            nc.vector.tensor_scalar(xpair[:, m, :], pair[:, m, :], xzn[:, m : m + 1], None, ALU.mult)
+            nc.vector.scalar_tensor_tensor(f64n[m][:], e1n[m][:], 64.0, rec[m][:, 0:G], ALU.mult, ALU.mult)
+            nc.scalar.activation(kk[m][:], gz[m][:], ACT.Copy, scale=rec[m][:, G : G + 1])
+            nc.scalar.activation(kx[m][:], xzn[m][:], ACT.Copy, scale=kk[m][:])
         for m in range(TILES):
-            nc.vector.tensor_tensor(hn[m][:], xpn[m][:], q[m][:], ALU.mult)
-            nc.vector.scalar_tensor_tensor(t0[m][:], xg[m][:], xpair[:, m, 0:1], f64[m][:], ALU.add, ALU.mult, accum_out=t0_sum[:, m : m + 1])
+            nc.vector.scalar_tensor_tensor(t0[m][:], xs[m][:], 1.0, f64n[m][:], ALU.mult, ALU.mult, accum_out=t0_sum[m][:])
+            nc.scalar.activation(yn_row[m][:], t0_sum[m][:], ACT.Identity, scale=1.0 / 64.0, bias=kx[m][:])
+            nc.scalar.activation(pairs(tn2[m][:]), twice(t0[m][:]), ACT.Identity, bias=yn_row[m][:])
+            t_turned.append(psum.tile([P, P], F32, name=f"t_turned{m}", tag=f"bank_d{m}"))
+            nc.tensor.transpose(t_turned[m][:], tn2[m][:], ident[:])
+        hn_both = keep.tile([P, TILES, J], F32, name="hn_both", tag="den1")
+        hn = [hn_both[:, m, :] for m in range(TILES)]
         for m in range(TILES):
-            nc.vector.scalar_tensor_tensor(grouped(yn[m][:]), spread(e1[m][:]), c1[:, m : m + 1], grouped(hn[m][:]), ALU.subtract, ALU.mult)
-            nc.vector.tensor_scalar(y_row[:, m : m + 1], t0_sum[:, m : m + 1], 1.0 / 64.0, xpair[:, m, 1:2], ALU.mult, ALU.add)
+            nc.vector.tensor_tensor(hn[m], xpn[m][:], q[m][:], ALU.mult)
+        acc = [psum.tile([P, J], F32, name=f"acc{m}", tag=f"acc{m}") for m in range(TILES)]
         for m in range(TILES):
-            nc.vector.tensor_tensor(u[m][:], base_sb[m][:], yn[m][:], ALU.subtract)
-            nc.vector.scalar_tensor_tensor(grouped(v[m][:]), spread(t0[m][:]), y_row[:, m : m + 1], grouped(sig[m][:]), ALU.add, ALU.mult)
-            nc.vector.tensor_tensor(o[m][:], v[m][:], u[m][:], ALU.add)
-            nc.sync.dma_start(out[m * P : (m + 1) * P, :], o[m][:])
+            nc.vector.tensor_tensor(blocks(y[m][:]), blocks(hn[m]), each_block(d_turned[m][:]), ALU.mult)
+            for c in range(BLOCKS):
+                cols = slice(c * P, (c + 1) * P)
+                nc.tensor.matmul(acc[m][:, cols], y[m][:, cols], ident[:], start=(c == 0), stop=False, is_transpose=True)
+        for m in range(TILES):
+            nc.vector.scalar_tensor_tensor(blocks(v[m][:]), blocks(q[m][:]), 1.0, each_block(t_turned[m][:]), ALU.subtract, ALU.mult)
+            for c in range(BLOCKS):
+                cols = slice(c * P, (c + 1) * P)
+                nc.tensor.matmul(acc[m][:, cols], v[m][:, cols], ident[:], start=False, stop=(c == BLOCKS - 1), is_transpose=True)
+        for m, g0, g1 in ((0, 0, G), (1, 0, G // 2), (1, G // 2, G)):
+            cols = slice(g0 * 8, g1 * 8)
+            nc.vector.tensor_tensor(
+                o[m][:, cols].rearrange("p (g c h) -> p g c h", c=BLOCKS, h=HALF),
+                acc[m][:].rearrange("p (c g h) -> p g c h", c=BLOCKS, h=HALF)[:, g0:g1, :, :],
+                base_sb[m][:, cols].rearrange("p (g c h) -> p g c h", c=BLOCKS, h=HALF), ALU.add)
+            nc.sync.dma_start(out[m * P : (m + 1) * P, cols], o[m][:, cols])

@@ -24,6 +24,7 @@ TILES = I // P
 BLOCKS = J // P
 HALF = P // G
 LN_FLOOR = 2.0 ** -62
+HALVES = (slice(0, J // 2), slice(J // 2, J))
 
 
 def tile_attend_hvpairquota_kernel(tc, taba, dtab, tabb_words, tabb_scales, reserve, stake, base, offs, offs2, out):
@@ -72,6 +73,8 @@ def tile_attend_hvpairquota_kernel(tc, taba, dtab, tabb_words, tabb_scales, rese
 
         floor = keep.tile([P, 1], F32, name="floor")
         nc.vector.memset(floor[:], LN_FLOOR)
+        warm = keep.tile([P, 1], F32, name="warm")
+        nc.scalar.activation(warm[:], floor[:], ACT.Sigmoid)
 
         got_words = keep.tile([P, J], U16, name="got_words", align_bytes=64)
         got_scales = keep.tile([P, J], U8, name="got_scales", align_bytes=64)
@@ -108,10 +111,12 @@ def tile_attend_hvpairquota_kernel(tc, taba, dtab, tabb_words, tabb_scales, rese
         nc.vector.tensor_copy(got_words[:], words[:].indirect(list_b[:]))
         nc.vector.tensor_copy(got_scales[:], scales[:].indirect(list_b[:]))
         deal(b_words[:].bitcast(I32), got_words[:].bitcast(I32), 4)
-        gather("a", woven_a, 0)
+        early = keep.tile([P, 2, I], F32, name="early")
+        nc.vector.tensor_copy(early[:, 0, :], planes["a", 0].indirect(list_a[:]))
         deal(b_scales[:].bitcast(U16), got_scales[:].bitcast(U16), 8)
-        for t in range(1, PACK - 1):
-            gather("a", woven_a, t)
+        nc.vector.tensor_copy(early[:, 1, :], planes["a", 1].indirect(list_a[:]))
+        nc.scalar.copy(woven_a[:, :, 0:2], early[:].rearrange("p t c -> p c t"))
+        gather("a", woven_a, 2)
         for m in range(TILES):
             gather("a", woven_a, PACK - 1, m)
         s = [scores("a", woven_a, m) for m in range(TILES)]
@@ -157,13 +162,14 @@ def tile_attend_hvpairquota_kernel(tc, taba, dtab, tabb_words, tabb_scales, rese
             return ap.rearrange("p (g h) -> p g h", h=HALF)
 
         def blocks(ap):
-            return ap.rearrange("p (c i) -> p c i", c=BLOCKS)
+            return ap.rearrange("p (c i) -> p c i", i=P)
 
-        def each_block(ap):
-            return ap.unsqueeze(1).to_broadcast([P, BLOCKS, P])
+        def each_block(ap, part=slice(0, J)):
+            return ap.unsqueeze(1).to_broadcast([P, (part.stop - part.start) // P, P])
 
         for m in range(TILES):
-            nc.vector.scalar_tensor_tensor(p[m], lnq[m][:], -1.0, s[m][:], ALU.mult, ALU.max)
+            for half in HALVES:
+                nc.vector.scalar_tensor_tensor(p[m][:, half], lnq[m][:, half], -1.0, s[m][:, half], ALU.mult, ALU.max)
             turn_sum(p_pairs[m][:], p[m])
         for m in range(TILES):
             nc.vector.scalar_tensor_tensor(xpn[m][:], q[m][:], 1.0, ts[m][:], ALU.subtract, ALU.mult)
@@ -206,7 +212,9 @@ def tile_attend_hvpairquota_kernel(tc, taba, dtab, tabb_words, tabb_scales, rese
                 cols = slice(c * P, (c + 1) * P)
                 nc.tensor.matmul(acc[m][:, cols], y[m][:, cols], ident[:], start=(c == 0), stop=False, is_transpose=True)
         for m in range(TILES):
-            nc.vector.scalar_tensor_tensor(blocks(v[m][:]), blocks(q[m][:]), 1.0, each_block(t_turned[m][:]), ALU.subtract, ALU.mult)
+            for part in (HALVES if m == TILES - 1 else (slice(0, J),)):
+                nc.vector.scalar_tensor_tensor(
+                    blocks(v[m][:, part]), blocks(q[m][:, part]), 1.0, each_block(t_turned[m][:], part), ALU.subtract, ALU.mult)
             for c in range(BLOCKS):
                 cols = slice(c * P, (c + 1) * P)
                 nc.tensor.matmul(acc[m][:, cols], v[m][:, cols], ident[:], start=False, stop=(c == BLOCKS - 1), is_transpose=True)

from contextlib import ExitStack

import concourse.mybir as mybir
from concourse.masks import make_identity

D, T, U, I, J, G = 512, 1024, 1024, 256, 512, 64
FLOPS = 2 * 2 * D * I * J

F32 = mybir.dt.float32
BF16 = mybir.dt.bfloat16
I32 = mybir.dt.int32
U32 = mybir.dt.uint32
U16 = mybir.dt.uint16
U8 = mybir.dt.uint8
FP8X4 = mybir.dt.float8_e4m3fn_x4
FP4X4 = mybir.dt.float4_e2m1fn_x4
ALU = mybir.AluOpType
ACT = mybir.ActivationFunctionType
AX = mybir.AxisListType

P = 128
PACK = 4
TILES = I // P
BLOCKS = J // P
HALF = P // G
LN_FLOOR = 2.0 ** -62
HALVES = (slice(0, J // 2), slice(J // 2, J))


def tile_attend_hvpairquota_kernel(tc, taba, dtab, tabb_words, tabb_scales, reserve, stake, base, offs, offs2, out):
    nc = tc.nc
    with ExitStack() as ctx:
        keep = ctx.enter_context(tc.tile_pool(name="keep", bufs=1))
        psum = ctx.enter_context(tc.psum_pool(name="psum", bufs=1))

        scales = keep.tile([P, U], U8, name="scales", align_bytes=64)
        nc.gpsimd.memset(scales[:].bitcast(I32), 0)

        list_b = keep.tile([P, J // 16], U16, name="list_b")
        nc.sync.dma_start(list_b[:], offs2)
        words = keep.tile([P, U], U16, name="words", align_bytes=64)
        nc.sync.dma_start(words[:].bitcast(I32), tabb_words[0].bitcast(I32))
        list_a = keep.tile([P, I // 16], U16, name="list_a")
        nc.sync.dma_start(list_a[:], offs)

        for quad in range(4):
            nc.sync.dma_start(
                scales[32 * quad : 32 * quad + 4, :].bitcast(I32),
                tabb_scales[0, 4 * quad : 4 * quad + 4, :].bitcast(I32),
            )
        planes = {}
        rows_a = taba.rearrange("(p t) c -> p t c", t=PACK)
        rows_d = dtab.rearrange("(p t) c -> p t c", t=PACK)
        first_two = keep.tile([P, 2, T], F32, name="first_two")
        nc.sync.dma_start(first_two[:], rows_a[:, 0:2, :])
        planes["a", 0], planes["a", 1] = first_two[:, 0, :], first_two[:, 1, :]
        stake_sb = keep.tile([P, TILES, G], F32, name="stake_sb")
        nc.sync.dma_start(stake_sb[:], stake.rearrange("(m p) g -> p m g", p=P))
        for name, rows, first in (("a", rows_a, 2), ("d", rows_d, 0)):
            for t in range(first, PACK):
                plane_tile = keep.tile([P, T], F32, name=f"plane_{name}{t}")
                nc.sync.dma_start(plane_tile[:], rows[:, t, :])
                planes[name, t] = plane_tile[:]
        reserve_sb = keep.tile([P, TILES], F32, name="reserve_sb")
        with nc.allow_non_contiguous_dma(reason="one reserve a partition and tile"):
            nc.sync.dma_start(reserve_sb[:].unsqueeze(2), reserve.rearrange("(m p) o -> p m o", p=P))
        base_sb = [keep.tile([P, J], F32, name=f"base{m}") for m in range(TILES)]
        for m in range(TILES):
            nc.sync.dma_start(base_sb[m][:], base[m * P : (m + 1) * P, :])

        ident = keep.tile([P, P], F32, name="ident")
        make_identity(nc, ident[:])

        floor = keep.tile([P, 1], F32, name="floor")
        nc.vector.memset(floor[:], LN_FLOOR)
        warm = keep.tile([P, 1], F32, name="warm")
        nc.scalar.activation(warm[:], floor[:], ACT.Sigmoid)

        got_words = keep.tile([P, J], U16, name="got_words", align_bytes=64)
        got_scales = keep.tile([P, J], U8, name="got_scales", align_bytes=64)
        b_words = keep.tile([P, J], U16, name="b_words", align_bytes=64)
        b_scales = keep.tile([P, J], U8, name="b_scales", align_bytes=64)

        def deal(dst, src, run):
            nc.vector.tensor_copy(
                dst.rearrange("p (c b g) -> p b c g", c=BLOCKS, g=run), src.rearrange("p (b g c) -> p b c g", c=BLOCKS, g=run))

        def gather(name, woven, t, m=None):
            if m is None:
                nc.vector.tensor_copy(woven[:, :, t], planes[name, t].indirect(list_a[:]))
            else:
                nc.vector.tensor_copy(woven[:, m * P : (m + 1) * P, t], planes[name, t].indirect(list_a[:, m * 8 : (m + 1) * 8]))

        def scores(name, woven, m):
            codes = keep.tile([P, P], U32, name=f"codes_{name}{m}", align_bytes=64)
            plane = keep.tile([P, P], U8, name=f"scale_{name}{m}", align_bytes=64)
            nc.vector.quantize_mx(
                out=codes[:].bitcast(FP8X4), scales=plane[:],
                in_=woven[:, m * P : (m + 1) * P, :].rearrange("p c t -> p (c t)"))
            bank = psum.tile([P, J], F32, name=f"bank_{name}{m}", tag=f"bank_{name}{m}")
            for c in range(BLOCKS):
                cols = slice(c * P, (c + 1) * P)
                nc.tensor.matmul_mx(
                    out=bank[:, cols], lhsT=b_words[:, cols].bitcast(FP4X4), lhsT_scale=b_scales[:, cols],
                    rhs=codes[:].bitcast(FP8X4), rhs_scale=plane[:], start=True, stop=True,
                )
            return bank

        woven_a = keep.tile([P, I, PACK], BF16, name="woven_a", align_bytes=64)
        woven_d = keep.tile([P, I, PACK], BF16, name="woven_d", tag="woven_d", align_bytes=64)
        nc.vector.tensor_copy(got_words[:], words[:].indirect(list_b[:]))
        nc.vector.tensor_copy(got_scales[:], scales[:].indirect(list_b[:]))
        deal(b_words[:].bitcast(I32), got_words[:].bitcast(I32), 4)
        early = keep.tile([P, 2, I], F32, name="early")
        nc.vector.tensor_copy(early[:, 0, :], planes["a", 0].indirect(list_a[:]))
        deal(b_scales[:].bitcast(U16), got_scales[:].bitcast(U16), 8)
        nc.vector.tensor_copy(early[:, 1, :], planes["a", 1].indirect(list_a[:]))
        nc.scalar.copy(woven_a[:, :, 0:2], early[:].rearrange("p t c -> p c t"))
        gather("a", woven_a, 2)
        for m in range(TILES):
            gather("a", woven_a, PACK - 1, m)
        s = [scores("a", woven_a, m) for m in range(TILES)]

        def tiles(name, width):
            return [keep.tile([P, width], F32, name=f"{name}{m}", tag=f"{name}{m}") for m in range(TILES)]

        q, lnq = tiles("q", J), tiles("lnq", J)
        stake8, stake8_sum = tiles("stake8", G), tiles("stake8_sum", 1)
        for m in range(TILES):
            nc.scalar.activation(stake8[m][:], stake_sb[:, m, :], ACT.Copy, scale=8.0, accum_out=stake8_sum[m][:])
        for m in range(TILES):
            nc.scalar.activation(q[m][:], s[m][:], ACT.Sigmoid, scale=-1.0)
        for m in range(TILES):
            nc.scalar.activation(lnq[m][:], q[m][:], ACT.Ln, bias=floor[:])

        for t in range(PACK - 1):
            gather("d", woven_d, t)
        for m in range(TILES):
            gather("d", woven_d, PACK - 1, m)
        ts = [scores("d", woven_d, m) for m in range(TILES)]

        def turn_sum(dst, src):
            for c in range(BLOCKS):
                nc.tensor.matmul(dst, src[:, c * P : (c + 1) * P], ident[:], start=(c == 0), stop=(c == BLOCKS - 1), is_transpose=True)

        p_both = keep.tile([P, TILES, J], F32, name="p_both", tag="woven_d", align_bytes=64)
        p = [p_both[:, m, :] for m in range(TILES)]
        xpn, y, v, o = (tiles(n, J) for n in ("xpn", "y", "v", "o"))
        p64, xh, dn2, tn2 = (tiles(n, P) for n in ("p64", "xh", "dn2", "tn2"))
        den, rec = tiles("den", G + 1), tiles("rec", G + 1)
        e1n, f64n, xs, t0 = (tiles(n, G) for n in ("e1n", "f64n", "xs", "t0"))
        p64_sum, e1n_sum, gz, kk, cn, xzn, xzn64, kx, t0_sum, yn_row = (
            tiles(n, 1) for n in ("p64_sum", "e1n_sum", "gz", "kk", "cn", "xzn", "xzn64", "kx", "t0_sum", "yn_row"))
        p_pairs = [psum.tile([P, P], F32, name=f"p_pairs{m}") for m in range(TILES)]
        x_pairs = [psum.tile([P, P], F32, name=f"x_pairs{m}", tag=f"acc{m}") for m in range(TILES)]
        d_turned, t_turned = [], []

        def twice(ap):
            return ap.unsqueeze(2).to_broadcast([P, G, HALF])

        def pairs(ap):
            return ap.rearrange("p (g h) -> p g h", h=HALF)

        def blocks(ap):
            return ap.rearrange("p (c i) -> p c i", i=P)

        def each_block(ap, part=slice(0, J)):
            return ap.unsqueeze(1).to_broadcast([P, (part.stop - part.start) // P, P])

        for m in range(TILES):
            for half in HALVES:
                nc.vector.scalar_tensor_tensor(p[m][:, half], lnq[m][:, half], -1.0, s[m][:, half], ALU.mult, ALU.max)
            turn_sum(p_pairs[m][:], p[m])
        for m in range(TILES):
            nc.vector.scalar_tensor_tensor(xpn[m][:], q[m][:], 1.0, ts[m][:], ALU.subtract, ALU.mult)
            turn_sum(x_pairs[m][:], xpn[m])
        for m in range(TILES):
            nc.scalar.activation(p64[m][:], p_pairs[m][:], ACT.Copy, scale=64.0, accum_out=p64_sum[m][:])
            nc.scalar.activation(den[m][:, G : G + 1], p64_sum[m][:], ACT.Identity, scale=1.0 / 64.0, bias=reserve_sb[:, m : m + 1])
            nc.vector.scalar_tensor_tensor(den[m][:, 0:G], p64[m][:, 0::2], den[m][:, G : G + 1], p64[m][:, 1::2], ALU.add, ALU.add)
        for m in range(TILES):
            nc.vector.reciprocal(rec[m][:], den[m][:])
        for m in range(TILES):
            nc.scalar.activation(xh[m][:], x_pairs[m][:], ACT.Copy, accum_out=xzn[m][:])
            nc.scalar.activation(xzn64[m][:], xzn[m][:], ACT.Copy, scale=1.0 / 64.0)
            nc.vector.scalar_tensor_tensor(xs[m][:], xh[m][:, 0::2], xzn64[m][:], xh[m][:, 1::2], ALU.add, ALU.add)
        for m in range(TILES):
            nc.vector.scalar_tensor_tensor(e1n[m][:], stake8[m][:], -64.0, rec[m][:, 0:G], ALU.mult, ALU.mult, accum_out=e1n_sum[m][:])
            nc.scalar.activation(gz[m][:], stake8_sum[m][:], ACT.Copy, scale=rec[m][:, G : G + 1])
            nc.scalar.activation(cn[m][:], e1n_sum[m][:], ACT.Identity, scale=1.0 / 64.0, bias=gz[m][:])
            nc.scalar.activation(pairs(dn2[m][:]), twice(e1n[m][:]), ACT.Identity, bias=cn[m][:])
            d_turned.append(psum.tile([P, P], F32, name=f"d_turned{m}", tag=f"bank_a{m}"))
            nc.tensor.transpose(d_turned[m][:], dn2[m][:], ident[:])
        for m in range(TILES):
            nc.vector.scalar_tensor_tensor(f64n[m][:], e1n[m][:], 64.0, rec[m][:, 0:G], ALU.mult, ALU.mult)
            nc.scalar.activation(kk[m][:], gz[m][:], ACT.Copy, scale=rec[m][:, G : G + 1])
            nc.scalar.activation(kx[m][:], xzn[m][:], ACT.Copy, scale=kk[m][:])
        for m in range(TILES):
            nc.vector.scalar_tensor_tensor(t0[m][:], xs[m][:], 1.0, f64n[m][:], ALU.mult, ALU.mult, accum_out=t0_sum[m][:])
            nc.scalar.activation(yn_row[m][:], t0_sum[m][:], ACT.Identity, scale=1.0 / 64.0, bias=kx[m][:])
            nc.scalar.activation(pairs(tn2[m][:]), twice(t0[m][:]), ACT.Identity, bias=yn_row[m][:])
            t_turned.append(psum.tile([P, P], F32, name=f"t_turned{m}", tag=f"bank_d{m}"))
            nc.tensor.transpose(t_turned[m][:], tn2[m][:], ident[:])
        hn_both = keep.tile([P, TILES, J], F32, name="hn_both", tag="den1")
        hn = [hn_both[:, m, :] for m in range(TILES)]
        for m in range(TILES):
            nc.vector.tensor_tensor(hn[m], xpn[m][:], q[m][:], ALU.mult)
        acc = [psum.tile([P, J], F32, name=f"acc{m}", tag=f"acc{m}") for m in range(TILES)]
        for m in range(TILES):
            nc.vector.tensor_tensor(blocks(y[m][:]), blocks(hn[m]), each_block(d_turned[m][:]), ALU.mult)
            for c in range(BLOCKS):
                cols = slice(c * P, (c + 1) * P)
                nc.tensor.matmul(acc[m][:, cols], y[m][:, cols], ident[:], start=(c == 0), stop=False, is_transpose=True)
        for m in range(TILES):
            for part in (HALVES if m == TILES - 1 else (slice(0, J),)):
                nc.vector.scalar_tensor_tensor(
                    blocks(v[m][:, part]), blocks(q[m][:, part]), 1.0, each_block(t_turned[m][:], part), ALU.subtract, ALU.mult)
            for c in range(BLOCKS):
                cols = slice(c * P, (c + 1) * P)
                nc.tensor.matmul(acc[m][:, cols], v[m][:, cols], ident[:], start=False, stop=(c == BLOCKS - 1), is_transpose=True)
        for m, g0, g1 in ((0, 0, G), (1, 0, G // 2), (1, G // 2, G)):
            cols = slice(g0 * 8, g1 * 8)
            nc.vector.tensor_tensor(
                o[m][:, cols].rearrange("p (g c h) -> p g c h", c=BLOCKS, h=HALF),
                acc[m][:].rearrange("p (c g h) -> p g c h", c=BLOCKS, h=HALF)[:, g0:g1, :, :],
                base_sb[m][:, cols].rearrange("p (g c h) -> p g c h", c=BLOCKS, h=HALF), ALU.add)
            nc.sync.dma_start(out[m * P : (m + 1) * P, cols], o[m][:, cols])
